import numpy as np
import ml_dtypes


def mxq(x, axis, fmt="e4m3"):
    dtype, down = {"e4m3": (ml_dtypes.float8_e4m3fn, 7), "e5m2": (ml_dtypes.float8_e5m2, 14)}[fmt]
    v = np.moveaxis(np.asarray(x, np.float32).astype(ml_dtypes.bfloat16).astype(np.float64), axis, -1)
    blocks = v.reshape(v.shape[:-1] + (-1, 32))
    amax = np.abs(blocks).max(-1, keepdims=True)
    byte = np.maximum(np.where(amax > 0, np.frexp(amax)[1] - 1 + 127, 0) - down, 1)
    scale = np.exp2(byte - 127.0)
    codes = (blocks / scale).astype(np.float32).astype(dtype).astype(np.float64)
    return np.moveaxis((codes * scale).reshape(v.shape), -1, axis)


WIDE = False


def mx_kscale(k):
    if not WIDE:
        return np.ones(k)
    levels = np.array([10, -10, 5, -5, 0])
    if k % 512:
        return np.exp2(np.random.permutation(np.resize(levels, k // 32))).repeat(32)
    a = np.empty((k // 512, 16))
    for p in range(k // 512):
        a[p, :8] = np.random.permutation(np.resize(levels, 8))
        for g in range(8):
            far = levels[np.abs(levels - a[p, g]) >= 10]
            a[p, g + 8] = far[np.random.randint(len(far))]
    return np.exp2(a.ravel()).repeat(32)


BF16 = ml_dtypes.bfloat16


def bf(x):
    return np.asarray(x, np.float32).astype(BF16)


def f64(x):
    return np.asarray(x).astype(np.float64)


E2M1 = np.array([0.0, 0.5, 1.0, 1.5, 2.0, 3.0, 4.0, 6.0, -0.0, -0.5, -1.0, -1.5, -2.0, -3.0, -4.0, -6.0])


def pack_weight(w, fmt):
    k, n = w.shape
    w = f64(bf(w)).reshape(k // 32, 32, n)
    amax = np.abs(w).max(1)
    if fmt == "e4m3":
        byte = np.frexp(amax)[1] - 1 + 127 - 7
    else:
        mant, ex = np.frexp(amax / 6.0)
        byte = np.where(mant > 0.5, ex, ex - 1) + 127
    byte = np.clip(np.where(amax > 0, byte, 1), 1, 254)
    scaled = (w * np.exp2(127.0 - byte)[:, None, :]).reshape(k, n).astype(np.float32)
    by_word = np.ascontiguousarray(scaled.reshape(k // 512, 128, 4, n).transpose(0, 1, 3, 2))
    if fmt == "e4m3":
        words = by_word.astype(ml_dtypes.float8_e4m3fn).view(np.uint8)
    else:
        c = by_word.astype(ml_dtypes.float4_e2m1fn).view(np.uint8) & 0xF
        words = c[..., 0::2] | (c[..., 1::2] << 4)
    return np.ascontiguousarray(words), np.ascontiguousarray(byte.astype(np.uint8).reshape(k // 512, 16, n))


def unpack_weight(words, scales, fmt):
    g, p, n, _ = words.shape
    if fmt == "e4m3":
        vals = np.ascontiguousarray(words).view(ml_dtypes.float8_e4m3fn).astype(np.float64)
    else:
        nib = np.empty((g, p, n, 4), np.uint8)
        nib[..., 0::2] = words & 0xF
        nib[..., 1::2] = words >> 4
        vals = E2M1[nib]
    vals = vals * np.repeat(np.exp2(scales.astype(np.float64) - 127.0), 8, axis=1)[..., None]
    return vals.transpose(0, 1, 3, 2).reshape(g * 512, n)
def pack4(w):
    words, scales = pack_weight(w, "e2m1")
    return words.reshape(words.shape[0], 128, -1), scales


def unpack4(words, scales):
    return unpack_weight(words.reshape(words.shape[0], 128, -1, 2), scales, "e2m1")


M, E, C = 1024, 4096, 512

LOW = 0.4
MOMENTUM = 0.5


def setup_inputs():
    s = mx_kscale(E)
    high = np.random.standard_normal((M, E)) / np.sqrt(E) / s
    low = LOW * np.random.standard_normal((E, M)) / np.sqrt(E) / s[:, None]
    low_words, low_scales = pack4(low)
    return {"high": bf(high),
            "low_words": low_words,
            "low_scales": low_scales,
            "x": bf(np.random.standard_normal((E, C)) * s[:, None]),
            "rhs": bf(np.random.standard_normal((M, C))),
            "dinv": bf(1 + 0.1 * np.random.standard_normal(M)),
            "beta": bf(MOMENTUM + 0.1 * np.random.standard_normal(C)),
            "prev": bf(np.random.standard_normal((M, C)))}


def reference(high, low_words, low_scales, x, rhs, dinv, beta, prev):
    xq = mxq(f64(x), 0, "e4m3")
    hq = mxq(f64(high), 1, "e4m3")
    low = unpack4(low_words, low_scales)
    ax = (hq @ xq) + (low.T @ xq)
    res = f64(rhs) - ax
    step = f64(dinv)[:, None] * res + f64(beta) * f64(prev)
    return res, step

@@ -1,0 +1,346 @@
+from contextlib import ExitStack
+
+import concourse.mybir as mybir
+from concourse.masks import make_identity
+
+M, E, C = 1024, 4096, 512
+FLOPS = 2 * 2 * M * E * C
+
+F32 = mybir.dt.float32
+BF16 = mybir.dt.bfloat16
+U32 = mybir.dt.uint32
+I32 = mybir.dt.int32
+U8 = mybir.dt.uint8
+FP8X4 = mybir.dt.float8_e4m3fn_x4
+FP4X4 = mybir.dt.float4_e2m1fn_x4
+ALU = mybir.AluOpType
+
+P = 128
+K_PASS = 512
+PASSES = E // K_PASS
+TILES = M // P
+HALF = TILES // 2
+BLOCKS = 8
+X_SPLIT = 320
+
+
+def tile_sliced_residual_refinement_s1_kernel(
+    tc, high, low_words, low_scales, x, rhs, dinv, beta, prev, res_out, step_out
+):
+    nc = tc.nc
+    with ExitStack() as ctx:
+        keep = ctx.enter_context(tc.tile_pool(name="keep", bufs=1))
+        ring = ctx.enter_context(tc.tile_pool(name="ring", bufs=2))
+        psum = ctx.enter_context(tc.psum_pool(name="psum", bufs=1))
+        ctx.enter_context(tc.manual_schedule())
+
+        ident_f = keep.tile([P, P], F32, name="ident_f")
+        ident_b = keep.tile([P, P], BF16, name="ident_b")
+        cst = keep.tile([P, P], BF16, name="cst")
+        warm = keep.tile([P, 2], F32, name="warm")
+        nc.vector.memset(cst[:], 0.0)
+        nc.vector.memset(warm[:], 0.0)
+        nc.scalar.dma_start(out=cst[0:8, :], in_=dinv.rearrange("(t p) -> t p", p=P))
+        nc.scalar.dma_start(out=cst[8:12, :], in_=beta.rearrange("(q p) -> q p", p=P))
+        nc.scalar.copy(out=warm[:, 0:1], in_=warm[:, 1:2])
+        make_identity(nc, ident_b[:])
+        make_identity(nc, ident_f[:])
+
+        sc = []
+        for h in range(2):
+            s = keep.tile([P, PASSES, HALF * P], U8, name="sc%d" % h, align_bytes=64)
+            nc.vector.memset(s[:].rearrange("p g n -> p (g n)").bitcast(U32), 0)
+            sc.append(s)
+
+        x_raw = {}
+
+        def load_x(g):
+            t = ring.tile([P, 4, C], BF16, name="x_raw", bufs=6, align_bytes=64)
+            nc.sync.dma_start(
+                out=t[:], in_=x[g * K_PASS : (g + 1) * K_PASS, :].rearrange("(p j) c -> p j c", j=4)
+            )
+            x_raw[g] = t
+
+        h_raw = {}
+
+        def load_high_a(b, i):
+            t = keep.tile([P, 2 * K_PASS], BF16, name="ha_%d_%d" % (b, i), align_bytes=64)
+            nc.sync.dma_start(
+                out=t[:], in_=high[i * P : (i + 1) * P, b * 2 * K_PASS : (b + 1) * 2 * K_PASS]
+            )
+            h_raw[(b, i)] = t[:].bitcast(F32)
+
+        def load_high_b(m):
+            t = keep.tile([P, E], BF16, name="hb_%d" % m, align_bytes=64)
+            nc.sync.dma_start(out=t[:], in_=high[m * P : (m + 1) * P, :])
+            w = t[:].bitcast(F32)
+            for i in range(4):
+                h_raw[(m, i)] = w[:, i * K_PASS : (i + 1) * K_PASS]
+
+        low = {}
+
+        def load_low(half, g0, n):
+            w = HALF * P * 2
+            t = keep.tile([P, n, w], U8, name="low_%d_%d" % (half, g0), align_bytes=64)
+            nc.sync.dma_start(
+                out=t[:].bitcast(I32),
+                in_=low_words[g0 : g0 + n, :, half * w : (half + 1) * w]
+                .rearrange("g p n -> p g n")
+                .bitcast(I32),
+            )
+            for g in range(n):
+                low[(half, g0 + g)] = t[:, g, :]
+
+        def load_scales(half):
+            w = HALF * P
+            for q in range(4):
+                nc.sync.dma_start(
+                    out=sc[half][32 * q : 32 * q + 4, :, :].bitcast(I32),
+                    in_=low_scales[:, 4 * q : 4 * q + 4, half * w : (half + 1) * w]
+                    .rearrange("g q n -> q g n")
+                    .bitcast(I32),
+                )
+
+        rhs_t = {}
+        prev_t = {}
+
+        def load_rows(src, dst, half, name):
+            t = keep.tile([P, HALF, C], BF16, name="%s_%d" % (name, half), align_bytes=64)
+            nc.sync.dma_start(
+                out=t[:],
+                in_=src[half * HALF * P : (half + 1) * HALF * P, :].rearrange("(t p) c -> p t c", p=P),
+            )
+            for i in range(HALF):
+                dst[half * HALF + i] = t[:, i, :]
+
+        x_codes = {}
+        x_scales = {}
+        x_grp = {}
+
+        def x_interleave(g):
+            t = ring.tile([P, C, 4], BF16, name="x_grp", bufs=3, align_bytes=64)
+            for eng, c0, c1 in ((nc.vector.tensor_copy, 0, X_SPLIT), (nc.scalar.copy, X_SPLIT, C)):
+                eng(
+                    out=t[:, c0:c1, :].rearrange("p (c i) t -> p c t i", i=4),
+                    in_=x_raw[g][:, :, c0:c1].rearrange("p t (c i) -> p c t i", i=4),
+                )
+            x_grp[g] = t
+
+        def x_quant(g):
+            codes = keep.tile([P, C], U32, name="xc_%d" % g, align_bytes=64)
+            scales = keep.tile([P, C], U8, name="xs_%d" % g, align_bytes=64)
+            nc.vector.quantize_mx(
+                out=codes[:].bitcast(FP8X4),
+                scales=scales[:],
+                in_=x_grp[g][:].rearrange("p c t -> p (c t)"),
+            )
+            x_codes[g] = codes
+            x_scales[g] = scales
+
+        tr = {}
+
+        def transposes(b):
+            for i in range(4):
+                t = psum.tile([P, 2, 2, P], F32, name="tr", bufs=4)
+                for g in range(2):
+                    for u in range(2):
+                        nc.tensor.transpose(
+                            t[:, g, u, :],
+                            h_raw[(b, i)][:, 256 * g + u : 256 * (g + 1) : 2],
+                            ident_f[:],
+                        )
+                tr[(b, i)] = t
+
+        h_grp = {}
+        h_codes = {}
+        h_scales = {}
+
+        def evacuate(b, i):
+            t = ring.tile([P, 2, P, 4], BF16, name="h_grp", bufs=6, align_bytes=64)
+            nc.scalar.copy(
+                out=t[:].rearrange("p g m t -> p (g m t)").bitcast(F32).rearrange(
+                    "p (g m u) -> p g m u", g=2, u=2
+                ),
+                in_=tr[(b, i)][:].rearrange("p g u m -> p g m u"),
+            )
+            h_grp[(b, i)] = t
+
+        def h_quant(b, i):
+            codes = ring.tile([P, 2 * P], U32, name="hc", bufs=12, align_bytes=64)
+            scales = ring.tile([P, 2 * P], U8, name="hs", bufs=12, align_bytes=64)
+            nc.vector.quantize_mx(
+                out=codes[:].bitcast(FP8X4),
+                scales=scales[:],
+                in_=h_grp[(b, i)][:].rearrange("p g m t -> p (g m t)"),
+            )
+            h_codes[(b, i)] = codes
+            h_scales[(b, i)] = scales
+
+        acc = {}
+        started = {}
+
+        def mx(m, g, low_side, last):
+            if m not in acc:
+                acc[m] = psum.tile([P, C], F32, name="acc%d" % (m % HALF), bufs=1)
+                started[m] = False
+            if low_side:
+                half, i = divmod(m, HALF)
+                lhs = low[(half, g)][:, i * 2 * P : (i + 1) * 2 * P].bitcast(FP4X4)
+                lhs_s = sc[half][:, g, i * P : (i + 1) * P]
+            else:
+                key = (g // 2, m) if m < HALF else (m, g // 2)
+                cols = slice((g % 2) * P, (g % 2 + 1) * P)
+                lhs = h_codes[key][:, cols].bitcast(FP8X4)
+                lhs_s = h_scales[key][:, cols]
+            nc.tensor.matmul_mx(
+                out=acc[m][:],
+                lhsT=lhs,
+                lhsT_scale=lhs_s,
+                rhs=x_codes[g][:].bitcast(FP8X4),
+                rhs_scale=x_scales[g][:],
+                start=not started[m],
+                stop=last,
+            )
+            started[m] = True
+
+        bp = {}
+
+        def momentum(m):
+            t = ring.tile([P, C], F32, name="bp", bufs=4)
+            nc.vector.tensor_tensor(out=t[:], in0=prev_t[m], in1=beta_b[:], op=ALU.mult)
+            bp[m] = t
+
+        res_t = {}
+        step_t = {}
+
+        def epilogue(m):
+            r = ring.tile([P, C], F32, name="res", bufs=6)
+            s = ring.tile([P, C], F32, name="step", bufs=6)
+            nc.vector.tensor_tensor(out=r[:], in0=rhs_t[m], in1=acc[m][:], op=ALU.subtract)
+            nc.vector.scalar_tensor_tensor(
+                out=s[:], in0=r[:], scalar=dcol[:, m : m + 1], in1=bp[m][:], op0=ALU.mult, op1=ALU.add
+            )
+            res_t[m] = r
+            step_t[m] = s
+
+        def store(m):
+            nc.sync.dma_start(out=res_out[m * P : (m + 1) * P, :], in_=res_t[m][:])
+            nc.sync.dma_start(out=step_out[m * P : (m + 1) * P, :], in_=step_t[m][:])
+
+        load_x(0)
+        for i in range(4):
+            load_high_a(0, i)
+        load_low(0, 0, 2)
+        load_scales(0)
+        load_x(1)
+        def load_block_a(b):
+            for i in range(4):
+                load_high_a(b, i)
+            load_x(2 * b)
+            load_low(0, 2 * b, 2)
+            load_x(2 * b + 1)
+
+        load_block_a(1)
+
+        ct = psum.tile([P, 4 * P], BF16, name="tr", bufs=4)
+        nc.tensor.transpose(ct[:, 0:P], cst[:], ident_b[:])
+        dcol = keep.tile([P, 8], F32, name="dcol")
+        bcol = keep.tile([P, 4], BF16, name="bcol")
+        nc.scalar.copy(out=bcol[:], in_=ct[:, 8:12])
+        nc.scalar.copy(out=dcol[:], in_=ct[:, 0:8])
+        bt = psum.tile([P, 4 * P], BF16, name="tr", bufs=4)
+        for q in range(4):
+            nc.tensor.transpose(
+                bt[:, q * P : (q + 1) * P], bcol[:, q : q + 1].to_broadcast([P, P]), ident_b[:]
+            )
+        beta_b = keep.tile([P, C], BF16, name="beta_b")
+        nc.scalar.copy(out=beta_b[:], in_=bt[:])
+
+        x_interleave(0)
+        x_quant(0)
+        transposes(0)
+        for i in range(4):
+            evacuate(0, i)
+            h_quant(0, i)
+        x_interleave(1)
+        for i in range(4):
+            mx(i, 0, False, False)
+        for i in range(4):
+            mx(i, 0, True, False)
+        x_quant(1)
+        for i in range(4):
+            mx(i, 1, False, False)
+
+        for b in range(BLOCKS):
+            m_b = b
+            if b == 0:
+                pairs = []
+            elif b < HALF:
+                pairs = [(i, g) for g in (2 * b, 2 * b + 1) for i in range(HALF)]
+            else:
+                pairs = [(m_b, g) for g in range(PASSES)]
+            for m, g in pairs:
+                mx(m, g, True, False)
+
+            if b == 0:
+                load_block_a(2)
+            if b == 1:
+                load_block_a(3)
+                load_high_b(4)
+                load_low(1, 0, 4)
+                load_low(1, 4, 4)
+                load_scales(1)
+            if b == 2:
+                load_rows(prev, prev_t, 0, "prev")
+                load_rows(rhs, rhs_t, 0, "rhs")
+                load_high_b(5)
+                load_rows(prev, prev_t, 1, "prev")
+                load_rows(rhs, rhs_t, 1, "rhs")
+                load_high_b(6)
+                load_high_b(7)
+
+            if b + 1 < BLOCKS:
+                transposes(b + 1)
+            if b + 1 < HALF:
+                g0, g1 = 2 * b + 2, 2 * b + 3
+                x_interleave(g0)
+                evacuate(b + 1, 0)
+                evacuate(b + 1, 1)
+                h_quant(b + 1, 0)
+                x_quant(g0)
+                h_quant(b + 1, 1)
+                x_interleave(g1)
+                evacuate(b + 1, 2)
+                evacuate(b + 1, 3)
+                h_quant(b + 1, 2)
+                x_quant(g1)
+                h_quant(b + 1, 3)
+            elif b + 1 < BLOCKS:
+                for i in range(4):
+                    evacuate(b + 1, i)
+                    h_quant(b + 1, i)
+            if b == HALF - 1:
+                for i in range(HALF):
+                    momentum(i)
+            elif b >= HALF:
+                momentum(b)
+
+            if b == 0:
+                for i in range(4):
+                    mx(i, 1, True, False)
+            elif b < HALF - 1:
+                for g in (2 * b, 2 * b + 1):
+                    for i in range(HALF):
+                        mx(i, g, False, False)
+            elif b == HALF - 1:
+                for i in range(HALF):
+                    for g in (2 * b, 2 * b + 1):
+                        mx(i, g, False, g == PASSES - 1)
+                    epilogue(i)
+                for i in range(HALF):
+                    store(i)
+            else:
+                for g in range(PASSES):
+                    mx(b, g, False, g == PASSES - 1)
+                epilogue(b)
+                store(b)

@@ -4,6 +4,7 @@ import concourse.mybir as mybir
 from concourse.masks import make_identity
 
 M, E, C = 1024, 4096, 512
+PERMUTE = {2: "V", 3: "V", 4: "S", 5: "S", 6: "S", 7: "S"}
 FLOPS = 2 * 2 * M * E * C
 
 F32 = mybir.dt.float32
@@ -21,7 +22,7 @@ PASSES = E // K_PASS
 TILES = M // P
 HALF = TILES // 2
 BLOCKS = 8
-X_SPLIT = 320
+X_SPLIT = 384
 
 
 def tile_sliced_residual_refinement_s1_kernel(
@@ -137,6 +138,17 @@ def tile_sliced_residual_refinement_s1_kernel(
             x_codes[g] = codes
             x_scales[g] = scales
 
+        h_perm = {}
+
+        def permute(b):
+            if b not in PERMUTE:
+                return
+            for i in range(4):
+                t = ring.tile([P, 2, 2, P], F32, name="h_perm", bufs=8)
+                copy = nc.vector.tensor_copy if PERMUTE[b] == "V" else nc.scalar.copy
+                copy(out=t[:], in_=h_raw[(b, i)].rearrange("p (g m u) -> p g u m", g=2, u=2))
+                h_perm[(b, i)] = t
+
         tr = {}
 
         def transposes(b):
@@ -144,11 +156,11 @@ def tile_sliced_residual_refinement_s1_kernel(
                 t = psum.tile([P, 2, 2, P], F32, name="tr", bufs=4)
                 for g in range(2):
                     for u in range(2):
-                        nc.tensor.transpose(
-                            t[:, g, u, :],
-                            h_raw[(b, i)][:, 256 * g + u : 256 * (g + 1) : 2],
-                            ident_f[:],
-                        )
+                        if b in PERMUTE:
+                            src = h_perm[(b, i)][:, g, u, :]
+                        else:
+                            src = h_raw[(b, i)][:, 256 * g + u : 256 * (g + 1) : 2]
+                        nc.tensor.transpose(t[:, g, u, :], src, ident_f[:])
                 tr[(b, i)] = t
 
         h_grp = {}
@@ -166,8 +178,8 @@ def tile_sliced_residual_refinement_s1_kernel(
             h_grp[(b, i)] = t
 
         def h_quant(b, i):
-            codes = ring.tile([P, 2 * P], U32, name="hc", bufs=12, align_bytes=64)
-            scales = ring.tile([P, 2 * P], U8, name="hs", bufs=12, align_bytes=64)
+            codes = ring.tile([P, 2 * P], U32, name="hc", bufs=8, align_bytes=64)
+            scales = ring.tile([P, 2 * P], U8, name="hs", bufs=8, align_bytes=64)
             nc.vector.quantize_mx(
                 out=codes[:].bitcast(FP8X4),
                 scales=scales[:],
@@ -213,15 +225,23 @@ def tile_sliced_residual_refinement_s1_kernel(
         res_t = {}
         step_t = {}
 
-        def epilogue(m):
-            r = ring.tile([P, C], F32, name="res", bufs=6)
-            s = ring.tile([P, C], F32, name="step", bufs=6)
+        def residual(m):
+            r = ring.tile([P, C], F32, name="res", bufs=5)
             nc.vector.tensor_tensor(out=r[:], in0=rhs_t[m], in1=acc[m][:], op=ALU.subtract)
-            nc.vector.scalar_tensor_tensor(
-                out=s[:], in0=r[:], scalar=dcol[:, m : m + 1], in1=bp[m][:], op0=ALU.mult, op1=ALU.add
-            )
             res_t[m] = r
-            step_t[m] = s
+
+        def step(m, cols=slice(0, C)):
+            if m not in step_t:
+                s = ring.tile([P, C], F32, name="step", bufs=5)
+                step_t[m] = s
+            nc.vector.scalar_tensor_tensor(
+                out=step_t[m][:, cols],
+                in0=res_t[m][:, cols],
+                scalar=dcol[:, m : m + 1],
+                in1=bp[m][:, cols],
+                op0=ALU.mult,
+                op1=ALU.add,
+            )
 
         def store(m):
             nc.sync.dma_start(out=res_out[m * P : (m + 1) * P, :], in_=res_t[m][:])
@@ -256,91 +276,118 @@ def tile_sliced_residual_refinement_s1_kernel(
         beta_b = keep.tile([P, C], BF16, name="beta_b")
         nc.scalar.copy(out=beta_b[:], in_=bt[:])
 
+        def quant_block(b):
+            for i in range(4):
+                evacuate(b, i)
+                h_quant(b, i)
+
+        def finish(m):
+            momentum(m)
+            step(m)
+            store(m)
+
         x_interleave(0)
         x_quant(0)
         transposes(0)
-        for i in range(4):
-            evacuate(0, i)
-            h_quant(0, i)
+        quant_block(0)
         x_interleave(1)
-        for i in range(4):
-            mx(i, 0, False, False)
-        for i in range(4):
-            mx(i, 0, True, False)
         x_quant(1)
-        for i in range(4):
-            mx(i, 1, False, False)
+        permute(1)
+        for g in range(2):
+            for low_side in (False, True):
+                for i in range(HALF):
+                    mx(i, g, low_side, False)
 
-        for b in range(BLOCKS):
-            m_b = b
-            if b == 0:
-                pairs = []
-            elif b < HALF:
-                pairs = [(i, g) for g in (2 * b, 2 * b + 1) for i in range(HALF)]
-            else:
-                pairs = [(m_b, g) for g in range(PASSES)]
-            for m, g in pairs:
-                mx(m, g, True, False)
-
-            if b == 0:
-                load_block_a(2)
+        for b in range(1, HALF):
             if b == 1:
+                load_block_a(2)
+            if b == 2:
                 load_block_a(3)
+                load_rows(rhs, rhs_t, 0, "rhs")
                 load_high_b(4)
                 load_low(1, 0, 4)
-                load_low(1, 4, 4)
                 load_scales(1)
-            if b == 2:
+                load_low(1, 4, 4)
                 load_rows(prev, prev_t, 0, "prev")
-                load_rows(rhs, rhs_t, 0, "rhs")
                 load_high_b(5)
-                load_rows(prev, prev_t, 1, "prev")
-                load_rows(rhs, rhs_t, 1, "rhs")
                 load_high_b(6)
+                load_rows(rhs, rhs_t, 1, "rhs")
+                load_rows(prev, prev_t, 1, "prev")
                 load_high_b(7)
-
-            if b + 1 < BLOCKS:
-                transposes(b + 1)
-            if b + 1 < HALF:
-                g0, g1 = 2 * b + 2, 2 * b + 3
-                x_interleave(g0)
-                evacuate(b + 1, 0)
-                evacuate(b + 1, 1)
-                h_quant(b + 1, 0)
-                x_quant(g0)
-                h_quant(b + 1, 1)
-                x_interleave(g1)
-                evacuate(b + 1, 2)
-                evacuate(b + 1, 3)
-                h_quant(b + 1, 2)
-                x_quant(g1)
-                h_quant(b + 1, 3)
-            elif b + 1 < BLOCKS:
-                for i in range(4):
-                    evacuate(b + 1, i)
-                    h_quant(b + 1, i)
-            if b == HALF - 1:
-                for i in range(HALF):
-                    momentum(i)
-            elif b >= HALF:
-                momentum(b)
-
-            if b == 0:
-                for i in range(4):
-                    mx(i, 1, True, False)
-            elif b < HALF - 1:
+            transposes(b)
+            for g in (2 * b, 2 * b + 1):
+                x_interleave(g)
+                x_quant(g)
+            quant_block(b)
+            permute(b + 1)
+            if b < HALF - 1:
+                for g in (2 * b, 2 * b + 1):
+                    for low_side in (True, False):
+                        for i in range(HALF):
+                            mx(i, g, low_side, False)
+            else:
                 for g in (2 * b, 2 * b + 1):
                     for i in range(HALF):
-                        mx(i, g, False, False)
-            elif b == HALF - 1:
+                        mx(i, g, True, False)
                 for i in range(HALF):
                     for g in (2 * b, 2 * b + 1):
                         mx(i, g, False, g == PASSES - 1)
-                    epilogue(i)
-                for i in range(HALF):
-                    store(i)
-            else:
-                for g in range(PASSES):
-                    mx(b, g, False, g == PASSES - 1)
-                epilogue(b)
-                store(b)
+
+        transposes(4)
+        for i in range(4):
+            evacuate(4, i)
+        permute(5)
+        residual(0)
+        residual(1)
+        h_quant(4, 0)
+        residual(2)
+        h_quant(4, 1)
+        h_quant(4, 2)
+        residual(3)
+        h_quant(4, 3)
+
+        for m in range(HALF, TILES - 1):
+            for g in range(PASSES):
+                mx(m, g, True, False)
+            for g in range(PASSES):
+                mx(m, g, False, g == PASSES - 1)
+            transposes(m + 1)
+            if m == HALF:
+                finish(0)
+            quant_block(m + 1)
+            if m + 2 < BLOCKS:
+                permute(m + 2)
+            residual(m)
+            if m == HALF:
+                for i in range(1, HALF):
+                    finish(i)
+            finish(m)
+
+        m = TILES - 1
+        momentum(m)
+        for g in range(PASSES):
+            mx(m, g, True, g == PASSES - 1)
+        part = ring.tile([P, C], F32, name="part", bufs=1)
+        nc.vector.tensor_tensor(out=part[:], in0=rhs_t[m], in1=acc[m][:], op=ALU.subtract)
+        res_last = ring.tile([P, C], F32, name="res", bufs=5)
+        res_t[m] = res_last
+        for h in range(2):
+            cols = slice(h * 256, (h + 1) * 256)
+            acc_h = psum.tile([P, 256], F32, name="tr", bufs=4)
+            for g in range(PASSES):
+                lc = slice((g % 2) * P, (g % 2 + 1) * P)
+                nc.tensor.matmul_mx(
+                    out=acc_h[:],
+                    lhsT=h_codes[(m, g // 2)][:, lc].bitcast(FP8X4),
+                    lhsT_scale=h_scales[(m, g // 2)][:, lc],
+                    rhs=x_codes[g][:, cols].bitcast(FP8X4),
+                    rhs_scale=x_scales[g][:, cols],
+                    start=(g == 0),
+                    stop=(g == PASSES - 1),
+                )
+            nc.vector.tensor_tensor(
+                out=res_last[:, cols], in0=part[:, cols], in1=acc_h[:], op=ALU.subtract
+            )
+            nc.sync.dma_start(out=res_out[m * P : (m + 1) * P, cols], in_=res_last[:, cols])
+            step(m, cols)
+            nc.sync.dma_start(out=step_out[m * P : (m + 1) * P, cols], in_=step_t[m][:, cols])

@@ -4,7 +4,7 @@ import concourse.mybir as mybir
 from concourse.masks import make_identity
 
 M, E, C = 1024, 4096, 512
-PERMUTE = {2: "V", 3: "V", 4: "S", 5: "S", 6: "S", 7: "S"}
+PERMUTE = {1: "SSSS", 2: "VSVS", 3: "VSVS", 4: "SSSS", 5: "SSSS", 6: "SSSS", 7: "SSSS"}
 FLOPS = 2 * 2 * M * E * C
 
 F32 = mybir.dt.float32
@@ -22,7 +22,7 @@ PASSES = E // K_PASS
 TILES = M // P
 HALF = TILES // 2
 BLOCKS = 8
-X_SPLIT = 384
+X_SPLIT = 352
 
 
 def tile_sliced_residual_refinement_s1_kernel(
@@ -145,7 +145,7 @@ def tile_sliced_residual_refinement_s1_kernel(
                 return
             for i in range(4):
                 t = ring.tile([P, 2, 2, P], F32, name="h_perm", bufs=8)
-                copy = nc.vector.tensor_copy if PERMUTE[b] == "V" else nc.scalar.copy
+                copy = nc.vector.tensor_copy if PERMUTE[b][i] == "V" else nc.scalar.copy
                 copy(out=t[:], in_=h_raw[(b, i)].rearrange("p (g m u) -> p g u m", g=2, u=2))
                 h_perm[(b, i)] = t
 
@@ -230,18 +230,12 @@ def tile_sliced_residual_refinement_s1_kernel(
             nc.vector.tensor_tensor(out=r[:], in0=rhs_t[m], in1=acc[m][:], op=ALU.subtract)
             res_t[m] = r
 
-        def step(m, cols=slice(0, C)):
-            if m not in step_t:
-                s = ring.tile([P, C], F32, name="step", bufs=5)
-                step_t[m] = s
+        def step(m):
+            s = ring.tile([P, C], F32, name="step", bufs=5)
             nc.vector.scalar_tensor_tensor(
-                out=step_t[m][:, cols],
-                in0=res_t[m][:, cols],
-                scalar=dcol[:, m : m + 1],
-                in1=bp[m][:, cols],
-                op0=ALU.mult,
-                op1=ALU.add,
+                out=s[:], in0=res_t[m][:], scalar=dcol[:, m : m + 1], in1=bp[m][:], op0=ALU.mult, op1=ALU.add
             )
+            step_t[m] = s
 
         def store(m):
             nc.sync.dma_start(out=res_out[m * P : (m + 1) * P, :], in_=res_t[m][:])
@@ -250,9 +244,10 @@ def tile_sliced_residual_refinement_s1_kernel(
         load_x(0)
         for i in range(4):
             load_high_a(0, i)
+        load_x(1)
         load_low(0, 0, 2)
         load_scales(0)
-        load_x(1)
+
         def load_block_a(b):
             for i in range(4):
                 load_high_a(b, i)
@@ -262,29 +257,39 @@ def tile_sliced_residual_refinement_s1_kernel(
 
         load_block_a(1)
 
-        ct = psum.tile([P, 4 * P], BF16, name="tr", bufs=4)
-        nc.tensor.transpose(ct[:, 0:P], cst[:], ident_b[:])
         dcol = keep.tile([P, 8], F32, name="dcol")
+        ndcol = keep.tile([P, 8], F32, name="ndcol")
         bcol = keep.tile([P, 4], BF16, name="bcol")
-        nc.scalar.copy(out=bcol[:], in_=ct[:, 8:12])
-        nc.scalar.copy(out=dcol[:], in_=ct[:, 0:8])
-        bt = psum.tile([P, 4 * P], BF16, name="tr", bufs=4)
-        for q in range(4):
-            nc.tensor.transpose(
-                bt[:, q * P : (q + 1) * P], bcol[:, q : q + 1].to_broadcast([P, P]), ident_b[:]
-            )
         beta_b = keep.tile([P, C], BF16, name="beta_b")
-        nc.scalar.copy(out=beta_b[:], in_=bt[:])
+
+        def turn_vectors():
+            ct = psum.tile([P, 4 * P], BF16, name="tr", bufs=4)
+            nc.tensor.transpose(ct[:, 0:P], cst[:], ident_b[:])
+            nc.scalar.copy(out=bcol[:], in_=ct[:, 8:12])
+            nc.scalar.copy(out=dcol[:], in_=ct[:, 0:8])
+            nc.scalar.activation(
+                out=ndcol[:], in_=ct[:, 0:8], func=mybir.ActivationFunctionType.Copy, scale=-1.0
+            )
+
+        def spread_beta():
+            bt = psum.tile([P, 4 * P], BF16, name="tr", bufs=4)
+            for q in range(4):
+                nc.tensor.transpose(
+                    bt[:, q * P : (q + 1) * P], bcol[:, q : q + 1].to_broadcast([P, P]), ident_b[:]
+                )
+            nc.scalar.copy(out=beta_b[:], in_=bt[:])
 
         def quant_block(b):
             for i in range(4):
                 evacuate(b, i)
                 h_quant(b, i)
 
-        def finish(m):
-            momentum(m)
-            step(m)
-            store(m)
+        def finish(*tiles):
+            for m in tiles:
+                momentum(m)
+            for m in tiles:
+                step(m)
+                store(m)
 
         x_interleave(0)
         x_quant(0)
@@ -293,8 +298,8 @@ def tile_sliced_residual_refinement_s1_kernel(
         x_interleave(1)
         x_quant(1)
         permute(1)
-        for g in range(2):
-            for low_side in (False, True):
+        for low_side in (False, True):
+            for g in range(2):
                 for i in range(HALF):
                     mx(i, g, low_side, False)
 
@@ -314,6 +319,10 @@ def tile_sliced_residual_refinement_s1_kernel(
                 load_rows(rhs, rhs_t, 1, "rhs")
                 load_rows(prev, prev_t, 1, "prev")
                 load_high_b(7)
+            if b == 1:
+                turn_vectors()
+            if b == 2:
+                spread_beta()
             transposes(b)
             for g in (2 * b, 2 * b + 1):
                 x_interleave(g)
@@ -321,8 +330,8 @@ def tile_sliced_residual_refinement_s1_kernel(
             quant_block(b)
             permute(b + 1)
             if b < HALF - 1:
-                for g in (2 * b, 2 * b + 1):
-                    for low_side in (True, False):
+                for low_side in (True, False):
+                    for g in (2 * b, 2 * b + 1):
                         for i in range(HALF):
                             mx(i, g, low_side, False)
             else:
@@ -338,13 +347,11 @@ def tile_sliced_residual_refinement_s1_kernel(
             evacuate(4, i)
         permute(5)
         residual(0)
+        for i in range(4):
+            h_quant(4, i)
         residual(1)
-        h_quant(4, 0)
         residual(2)
-        h_quant(4, 1)
-        h_quant(4, 2)
-        residual(3)
-        h_quant(4, 3)
+        finish(0, 1)
 
         for m in range(HALF, TILES - 1):
             for g in range(PASSES):
@@ -352,25 +359,42 @@ def tile_sliced_residual_refinement_s1_kernel(
             for g in range(PASSES):
                 mx(m, g, False, g == PASSES - 1)
             transposes(m + 1)
-            if m == HALF:
-                finish(0)
-            quant_block(m + 1)
+            for i in range(4):
+                evacuate(m + 1, i)
             if m + 2 < BLOCKS:
                 permute(m + 2)
+            h_quant(m + 1, 0)
+            h_quant(m + 1, 1)
             residual(m)
-            if m == HALF:
-                for i in range(1, HALF):
-                    finish(i)
-            finish(m)
+            h_quant(m + 1, 2)
+            h_quant(m + 1, 3)
+            if m == 4:
+                residual(3)
+                finish(2, 3)
+            elif m == 5:
+                finish(4, 5)
+                momentum(6)
+                momentum(7)
+            else:
+                step(6)
+                store(6)
 
         m = TILES - 1
-        momentum(m)
         for g in range(PASSES):
             mx(m, g, True, g == PASSES - 1)
         part = ring.tile([P, C], F32, name="part", bufs=1)
         nc.vector.tensor_tensor(out=part[:], in0=rhs_t[m], in1=acc[m][:], op=ALU.subtract)
         res_last = ring.tile([P, C], F32, name="res", bufs=5)
-        res_t[m] = res_last
+        step_last = ring.tile([P, C], F32, name="step", bufs=5)
+        part_step = ring.tile([P, C], F32, name="part_step", bufs=1)
+        nc.vector.scalar_tensor_tensor(
+            out=part_step[:],
+            in0=part[:],
+            scalar=dcol[:, m : m + 1],
+            in1=bp[m][:],
+            op0=ALU.mult,
+            op1=ALU.add,
+        )
         for h in range(2):
             cols = slice(h * 256, (h + 1) * 256)
             acc_h = psum.tile([P, 256], F32, name="tr", bufs=4)
@@ -389,5 +413,12 @@ def tile_sliced_residual_refinement_s1_kernel(
                 out=res_last[:, cols], in0=part[:, cols], in1=acc_h[:], op=ALU.subtract
             )
             nc.sync.dma_start(out=res_out[m * P : (m + 1) * P, cols], in_=res_last[:, cols])
-            step(m, cols)
-            nc.sync.dma_start(out=step_out[m * P : (m + 1) * P, cols], in_=step_t[m][:, cols])
+            nc.vector.scalar_tensor_tensor(
+                out=step_last[:, cols],
+                in0=acc_h[:],
+                scalar=ndcol[:, m : m + 1],
+                in1=part_step[:, cols],
+                op0=ALU.mult,
+                op1=ALU.add,
+            )
+            nc.sync.dma_start(out=step_out[m * P : (m + 1) * P, cols], in_=step_last[:, cols])

from contextlib import ExitStack

import concourse.mybir as mybir
from concourse.masks import make_identity

M, E, C = 1024, 4096, 512
PERMUTE = {1: "SSSS", 2: "VSVS", 3: "VSVS", 4: "SSSS", 5: "SSSS", 6: "SSSS", 7: "SSSS"}
FLOPS = 2 * 2 * M * E * C

F32 = mybir.dt.float32
BF16 = mybir.dt.bfloat16
U32 = mybir.dt.uint32
I32 = mybir.dt.int32
U8 = mybir.dt.uint8
FP8X4 = mybir.dt.float8_e4m3fn_x4
FP4X4 = mybir.dt.float4_e2m1fn_x4
ALU = mybir.AluOpType

P = 128
K_PASS = 512
PASSES = E // K_PASS
TILES = M // P
HALF = TILES // 2
BLOCKS = 8
X_SPLIT = 352


def tile_sliced_residual_refinement_s1_kernel(
    tc, high, low_words, low_scales, x, rhs, dinv, beta, prev, res_out, step_out
):
    nc = tc.nc
    with ExitStack() as ctx:
        keep = ctx.enter_context(tc.tile_pool(name="keep", bufs=1))
        ring = ctx.enter_context(tc.tile_pool(name="ring", bufs=2))
        psum = ctx.enter_context(tc.psum_pool(name="psum", bufs=1))
        ctx.enter_context(tc.manual_schedule())

        ident_f = keep.tile([P, P], F32, name="ident_f")
        ident_b = keep.tile([P, P], BF16, name="ident_b")
        cst = keep.tile([P, P], BF16, name="cst")
        warm = keep.tile([P, 2], F32, name="warm")
        nc.vector.memset(cst[:], 0.0)
        nc.vector.memset(warm[:], 0.0)
        nc.scalar.dma_start(out=cst[0:8, :], in_=dinv.rearrange("(t p) -> t p", p=P))
        nc.scalar.dma_start(out=cst[8:12, :], in_=beta.rearrange("(q p) -> q p", p=P))
        nc.scalar.copy(out=warm[:, 0:1], in_=warm[:, 1:2])
        make_identity(nc, ident_b[:])
        make_identity(nc, ident_f[:])

        sc = []
        for h in range(2):
            s = keep.tile([P, PASSES, HALF * P], U8, name="sc%d" % h, align_bytes=64)
            nc.vector.memset(s[:].rearrange("p g n -> p (g n)").bitcast(U32), 0)
            sc.append(s)

        x_raw = {}

        def load_x(g):
            t = ring.tile([P, 4, C], BF16, name="x_raw", bufs=6, align_bytes=64)
            nc.sync.dma_start(
                out=t[:], in_=x[g * K_PASS : (g + 1) * K_PASS, :].rearrange("(p j) c -> p j c", j=4)
            )
            x_raw[g] = t

        h_raw = {}

        def load_high_a(b, i):
            t = keep.tile([P, 2 * K_PASS], BF16, name="ha_%d_%d" % (b, i), align_bytes=64)
            nc.sync.dma_start(
                out=t[:], in_=high[i * P : (i + 1) * P, b * 2 * K_PASS : (b + 1) * 2 * K_PASS]
            )
            h_raw[(b, i)] = t[:].bitcast(F32)

        def load_high_b(m):
            t = keep.tile([P, E], BF16, name="hb_%d" % m, align_bytes=64)
            nc.sync.dma_start(out=t[:], in_=high[m * P : (m + 1) * P, :])
            w = t[:].bitcast(F32)
            for i in range(4):
                h_raw[(m, i)] = w[:, i * K_PASS : (i + 1) * K_PASS]

        low = {}

        def load_low(half, g0, n):
            w = HALF * P * 2
            t = keep.tile([P, n, w], U8, name="low_%d_%d" % (half, g0), align_bytes=64)
            nc.sync.dma_start(
                out=t[:].bitcast(I32),
                in_=low_words[g0 : g0 + n, :, half * w : (half + 1) * w]
                .rearrange("g p n -> p g n")
                .bitcast(I32),
            )
            for g in range(n):
                low[(half, g0 + g)] = t[:, g, :]

        def load_scales(half):
            w = HALF * P
            for q in range(4):
                nc.sync.dma_start(
                    out=sc[half][32 * q : 32 * q + 4, :, :].bitcast(I32),
                    in_=low_scales[:, 4 * q : 4 * q + 4, half * w : (half + 1) * w]
                    .rearrange("g q n -> q g n")
                    .bitcast(I32),
                )

        rhs_t = {}
        prev_t = {}

        def load_rows(src, dst, half, name):
            t = keep.tile([P, HALF, C], BF16, name="%s_%d" % (name, half), align_bytes=64)
            nc.sync.dma_start(
                out=t[:],
                in_=src[half * HALF * P : (half + 1) * HALF * P, :].rearrange("(t p) c -> p t c", p=P),
            )
            for i in range(HALF):
                dst[half * HALF + i] = t[:, i, :]

        x_codes = {}
        x_scales = {}
        x_grp = {}

        def x_interleave(g):
            t = ring.tile([P, C, 4], BF16, name="x_grp", bufs=3, align_bytes=64)
            for eng, c0, c1 in ((nc.vector.tensor_copy, 0, X_SPLIT), (nc.scalar.copy, X_SPLIT, C)):
                eng(
                    out=t[:, c0:c1, :].rearrange("p (c i) t -> p c t i", i=4),
                    in_=x_raw[g][:, :, c0:c1].rearrange("p t (c i) -> p c t i", i=4),
                )
            x_grp[g] = t

        def x_quant(g):
            codes = keep.tile([P, C], U32, name="xc_%d" % g, align_bytes=64)
            scales = keep.tile([P, C], U8, name="xs_%d" % g, align_bytes=64)
            nc.vector.quantize_mx(
                out=codes[:].bitcast(FP8X4),
                scales=scales[:],
                in_=x_grp[g][:].rearrange("p c t -> p (c t)"),
            )
            x_codes[g] = codes
            x_scales[g] = scales

        h_perm = {}

        def permute(b):
            if b not in PERMUTE:
                return
            for i in range(4):
                t = ring.tile([P, 2, 2, P], F32, name="h_perm", bufs=8)
                copy = nc.vector.tensor_copy if PERMUTE[b][i] == "V" else nc.scalar.copy
                copy(out=t[:], in_=h_raw[(b, i)].rearrange("p (g m u) -> p g u m", g=2, u=2))
                h_perm[(b, i)] = t

        tr = {}

        def transposes(b):
            for i in range(4):
                t = psum.tile([P, 2, 2, P], F32, name="tr", bufs=4)
                for g in range(2):
                    for u in range(2):
                        if b in PERMUTE:
                            src = h_perm[(b, i)][:, g, u, :]
                        else:
                            src = h_raw[(b, i)][:, 256 * g + u : 256 * (g + 1) : 2]
                        nc.tensor.transpose(t[:, g, u, :], src, ident_f[:])
                tr[(b, i)] = t

        h_grp = {}
        h_codes = {}
        h_scales = {}

        def evacuate(b, i):
            t = ring.tile([P, 2, P, 4], BF16, name="h_grp", bufs=6, align_bytes=64)
            nc.scalar.copy(
                out=t[:].rearrange("p g m t -> p (g m t)").bitcast(F32).rearrange(
                    "p (g m u) -> p g m u", g=2, u=2
                ),
                in_=tr[(b, i)][:].rearrange("p g u m -> p g m u"),
            )
            h_grp[(b, i)] = t

        def h_quant(b, i):
            codes = ring.tile([P, 2 * P], U32, name="hc", bufs=8, align_bytes=64)
            scales = ring.tile([P, 2 * P], U8, name="hs", bufs=8, align_bytes=64)
            nc.vector.quantize_mx(
                out=codes[:].bitcast(FP8X4),
                scales=scales[:],
                in_=h_grp[(b, i)][:].rearrange("p g m t -> p (g m t)"),
            )
            h_codes[(b, i)] = codes
            h_scales[(b, i)] = scales

        acc = {}
        started = {}

        def mx(m, g, low_side, last):
            if m not in acc:
                acc[m] = psum.tile([P, C], F32, name="acc%d" % (m % HALF), bufs=1)
                started[m] = False
            if low_side:
                half, i = divmod(m, HALF)
                lhs = low[(half, g)][:, i * 2 * P : (i + 1) * 2 * P].bitcast(FP4X4)
                lhs_s = sc[half][:, g, i * P : (i + 1) * P]
            else:
                key = (g // 2, m) if m < HALF else (m, g // 2)
                cols = slice((g % 2) * P, (g % 2 + 1) * P)
                lhs = h_codes[key][:, cols].bitcast(FP8X4)
                lhs_s = h_scales[key][:, cols]
            nc.tensor.matmul_mx(
                out=acc[m][:],
                lhsT=lhs,
                lhsT_scale=lhs_s,
                rhs=x_codes[g][:].bitcast(FP8X4),
                rhs_scale=x_scales[g][:],
                start=not started[m],
                stop=last,
            )
            started[m] = True

        bp = {}

        def momentum(m):
            t = ring.tile([P, C], F32, name="bp", bufs=4)
            nc.vector.tensor_tensor(out=t[:], in0=prev_t[m], in1=beta_b[:], op=ALU.mult)
            bp[m] = t

        res_t = {}
        step_t = {}

        def residual(m):
            r = ring.tile([P, C], F32, name="res", bufs=5)
            nc.vector.tensor_tensor(out=r[:], in0=rhs_t[m], in1=acc[m][:], op=ALU.subtract)
            res_t[m] = r

        def step(m):
            s = ring.tile([P, C], F32, name="step", bufs=5)
            nc.vector.scalar_tensor_tensor(
                out=s[:], in0=res_t[m][:], scalar=dcol[:, m : m + 1], in1=bp[m][:], op0=ALU.mult, op1=ALU.add
            )
            step_t[m] = s

        def store(m):
            nc.sync.dma_start(out=res_out[m * P : (m + 1) * P, :], in_=res_t[m][:])
            nc.sync.dma_start(out=step_out[m * P : (m + 1) * P, :], in_=step_t[m][:])

        load_x(0)
        for i in range(4):
            load_high_a(0, i)
        load_x(1)
        load_low(0, 0, 2)
        load_scales(0)

        def load_block_a(b):
            for i in range(4):
                load_high_a(b, i)
            load_x(2 * b)
            load_low(0, 2 * b, 2)
            load_x(2 * b + 1)

        load_block_a(1)

        dcol = keep.tile([P, 8], F32, name="dcol")
        ndcol = keep.tile([P, 8], F32, name="ndcol")
        bcol = keep.tile([P, 4], BF16, name="bcol")
        beta_b = keep.tile([P, C], BF16, name="beta_b")

        def turn_vectors():
            ct = psum.tile([P, 4 * P], BF16, name="tr", bufs=4)
            nc.tensor.transpose(ct[:, 0:P], cst[:], ident_b[:])
            nc.scalar.copy(out=bcol[:], in_=ct[:, 8:12])
            nc.scalar.copy(out=dcol[:], in_=ct[:, 0:8])
            nc.scalar.activation(
                out=ndcol[:], in_=ct[:, 0:8], func=mybir.ActivationFunctionType.Copy, scale=-1.0
            )

        def spread_beta():
            bt = psum.tile([P, 4 * P], BF16, name="tr", bufs=4)
            for q in range(4):
                nc.tensor.transpose(
                    bt[:, q * P : (q + 1) * P], bcol[:, q : q + 1].to_broadcast([P, P]), ident_b[:]
                )
            nc.scalar.copy(out=beta_b[:], in_=bt[:])

        def quant_block(b):
            for i in range(4):
                evacuate(b, i)
                h_quant(b, i)

        def finish(*tiles):
            for m in tiles:
                momentum(m)
            for m in tiles:
                step(m)
                store(m)

        x_interleave(0)
        x_quant(0)
        transposes(0)
        quant_block(0)
        x_interleave(1)
        x_quant(1)
        permute(1)
        for low_side in (False, True):
            for g in range(2):
                for i in range(HALF):
                    mx(i, g, low_side, False)

        for b in range(1, HALF):
            if b == 1:
                load_block_a(2)
            if b == 2:
                load_block_a(3)
                load_rows(rhs, rhs_t, 0, "rhs")
                load_high_b(4)
                load_low(1, 0, 4)
                load_scales(1)
                load_low(1, 4, 4)
                load_rows(prev, prev_t, 0, "prev")
                load_high_b(5)
                load_high_b(6)
                load_rows(rhs, rhs_t, 1, "rhs")
                load_rows(prev, prev_t, 1, "prev")
                load_high_b(7)
            if b == 1:
                turn_vectors()
            if b == 2:
                spread_beta()
            transposes(b)
            for g in (2 * b, 2 * b + 1):
                x_interleave(g)
                x_quant(g)
            quant_block(b)
            permute(b + 1)
            if b < HALF - 1:
                for low_side in (True, False):
                    for g in (2 * b, 2 * b + 1):
                        for i in range(HALF):
                            mx(i, g, low_side, False)
            else:
                for g in (2 * b, 2 * b + 1):
                    for i in range(HALF):
                        mx(i, g, True, False)
                for i in range(HALF):
                    for g in (2 * b, 2 * b + 1):
                        mx(i, g, False, g == PASSES - 1)

        transposes(4)
        for i in range(4):
            evacuate(4, i)
        permute(5)
        residual(0)
        for i in range(4):
            h_quant(4, i)
        residual(1)
        residual(2)
        finish(0, 1)

        for m in range(HALF, TILES - 1):
            for g in range(PASSES):
                mx(m, g, True, False)
            for g in range(PASSES):
                mx(m, g, False, g == PASSES - 1)
            transposes(m + 1)
            for i in range(4):
                evacuate(m + 1, i)
            if m + 2 < BLOCKS:
                permute(m + 2)
            h_quant(m + 1, 0)
            h_quant(m + 1, 1)
            residual(m)
            h_quant(m + 1, 2)
            h_quant(m + 1, 3)
            if m == 4:
                residual(3)
                finish(2, 3)
            elif m == 5:
                finish(4, 5)
                momentum(6)
                momentum(7)
            else:
                step(6)
                store(6)

        m = TILES - 1
        for g in range(PASSES):
            mx(m, g, True, g == PASSES - 1)
        part = ring.tile([P, C], F32, name="part", bufs=1)
        nc.vector.tensor_tensor(out=part[:], in0=rhs_t[m], in1=acc[m][:], op=ALU.subtract)
        res_last = ring.tile([P, C], F32, name="res", bufs=5)
        step_last = ring.tile([P, C], F32, name="step", bufs=5)
        part_step = ring.tile([P, C], F32, name="part_step", bufs=1)
        nc.vector.scalar_tensor_tensor(
            out=part_step[:],
            in0=part[:],
            scalar=dcol[:, m : m + 1],
            in1=bp[m][:],
            op0=ALU.mult,
            op1=ALU.add,
        )
        for h in range(2):
            cols = slice(h * 256, (h + 1) * 256)
            acc_h = psum.tile([P, 256], F32, name="tr", bufs=4)
            for g in range(PASSES):
                lc = slice((g % 2) * P, (g % 2 + 1) * P)
                nc.tensor.matmul_mx(
                    out=acc_h[:],
                    lhsT=h_codes[(m, g // 2)][:, lc].bitcast(FP8X4),
                    lhsT_scale=h_scales[(m, g // 2)][:, lc],
                    rhs=x_codes[g][:, cols].bitcast(FP8X4),
                    rhs_scale=x_scales[g][:, cols],
                    start=(g == 0),
                    stop=(g == PASSES - 1),
                )
            nc.vector.tensor_tensor(
                out=res_last[:, cols], in0=part[:, cols], in1=acc_h[:], op=ALU.subtract
            )
            nc.sync.dma_start(out=res_out[m * P : (m + 1) * P, cols], in_=res_last[:, cols])
            nc.vector.scalar_tensor_tensor(
                out=step_last[:, cols],
                in0=acc_h[:],
                scalar=ndcol[:, m : m + 1],
                in1=part_step[:, cols],
                op0=ALU.mult,
                op1=ALU.add,
            )
            nc.sync.dma_start(out=step_out[m * P : (m + 1) * P, cols], in_=step_last[:, cols])
